import numpy as np
import ml_dtypes


def mxq(x, axis, fmt="e4m3"):
    dtype, down = {"e4m3": (ml_dtypes.float8_e4m3fn, 7), "e5m2": (ml_dtypes.float8_e5m2, 14)}[fmt]
    v = np.moveaxis(np.asarray(x, np.float32).astype(ml_dtypes.bfloat16).astype(np.float64), axis, -1)
    blocks = v.reshape(v.shape[:-1] + (-1, 32))
    amax = np.abs(blocks).max(-1, keepdims=True)
    byte = np.maximum(np.where(amax > 0, np.frexp(amax)[1] - 1 + 127, 0) - down, 1)
    scale = np.exp2(byte - 127.0)
    codes = (blocks / scale).astype(np.float32).astype(dtype).astype(np.float64)
    return np.moveaxis((codes * scale).reshape(v.shape), -1, axis)


WIDE = False


def mx_kscale(k):
    if not WIDE:
        return np.ones(k)
    levels = np.array([10, -10, 5, -5, 0])
    if k % 512:
        return np.exp2(np.random.permutation(np.resize(levels, k // 32))).repeat(32)
    a = np.empty((k // 512, 16))
    for p in range(k // 512):
        a[p, :8] = np.random.permutation(np.resize(levels, 8))
        for g in range(8):
            far = levels[np.abs(levels - a[p, g]) >= 10]
            a[p, g + 8] = far[np.random.randint(len(far))]
    return np.exp2(a.ravel()).repeat(32)


def f64(x):
    return np.asarray(x).astype(np.float64)


def striped(idx):
    return np.tile(idx.reshape(-1, 16).T, (8, 1)).astype(np.uint16)


def unstriped(offs):
    return offs[:16].T.reshape(-1).astype(np.int64)


def silu(v):
    return v / (1.0 + np.exp(-np.maximum(v, -700.0)))


K, T, E, C, H, N = 512, 3072, 6, 256, 512, 256


def by_expert(wq, xq):
    return np.concatenate([wq[e].T @ xq[:, e * C:(e + 1) * C] for e in range(E)], axis=1)


def setup_inputs():
    n = np.random.standard_normal
    s = mx_kscale(K)[:, None]
    u = mx_kscale(H)
    return {
        "xT": (n((K, T)) * s).astype(np.float32),
        "w1": (n((E, K, H)) / np.sqrt(K) / s[None] * u[None, None, :]).astype(np.float32),
        "w2": (n((E, H, N)) / np.sqrt(H) / u[None, :, None]).astype(np.float32),
        "gate": np.tile(np.random.uniform(0.2, 1.0, E * C), (N, 1)).astype(np.float32),
        "offs": striped(np.random.permutation(T)[:E * C]),
    }


def reference(xT, w1, w2, gate, offs):
    idx = unstriped(offs)
    xq = mxq(f64(xT)[:, idx], 0, "e4m3")
    h = silu(by_expert(mxq(f64(w1), 1, "e4m3"), xq))
    y = by_expert(mxq(f64(w2), 1, "e4m3"), mxq(h, 0, "e4m3"))
    out = np.zeros((N, T))
    out[:, idx] = f64(gate) * y
    return out

@@ -1,0 +1,214 @@
+from contextlib import ExitStack
+
+import concourse.mybir as mybir
+
+K, T, E, C, H, N = 512, 3072, 6, 256, 512, 256
+SLOTS = E * C
+P = 128
+PACK = 4
+GROUP = 512
+CHUNK = 1024
+PIECES = ((0, 512), (512, 1152), (1152, 1536))
+HALF = 128
+
+FLOPS = 2 * SLOTS * H * (K + N)
+
+F32 = mybir.dt.float32
+BF16 = mybir.dt.bfloat16
+U32 = mybir.dt.uint32
+U16 = mybir.dt.uint16
+U8 = mybir.dt.uint8
+FP8X4 = mybir.dt.float8_e4m3fn_x4
+SILU = mybir.ActivationFunctionType.Silu
+MULT = mybir.AluOpType.mult
+
+
+def tile_routed_moe_kernel(tc, xT, w1, w2, gate, offs, out):
+    nc = tc.nc
+    with ExitStack() as ctx:
+        keep = ctx.enter_context(tc.tile_pool(name="keep", bufs=1))
+        raws = ctx.enter_context(tc.tile_pool(name="raws", bufs=10))
+        work = ctx.enter_context(tc.tile_pool(name="work", bufs=2))
+        psum_h = ctx.enter_context(tc.psum_pool(name="psum_h", bufs=4))
+        psum_y = ctx.enter_context(tc.psum_pool(name="psum_y", bufs=2))
+
+        offsets = keep.tile([P, SLOTS // 16], U16, name="offsets")
+        nc.sync.dma_start(offsets[:], offs)
+
+        warm_in = keep.tile([P, 8], F32, name="warm_in")
+        warm_out = keep.tile([P, 8], F32, name="warm_out")
+        nc.gpsimd.memset(warm_in[:], 0.0)
+        nc.scalar.activation(warm_out[:], warm_in[:], SILU)
+
+        x_view = xT.rearrange("(p u e) n -> u p e n", u=2, e=2)
+
+        def load_x(u, c):
+            raw = raws.tile([P, 2, CHUNK], F32, name="raw")
+            nc.sync.dma_start(raw[:], x_view[u, :, :, c * CHUNK : (c + 1) * CHUNK])
+            return raw
+
+        def load_w1(e):
+            raw = raws.tile([P, PACK, H], F32, name="raw")
+            nc.sync.dma_start(raw[:], w1[e].rearrange("(p j) i -> p j i", j=PACK))
+            return raw
+
+        def load_w2(pair):
+            raw = raws.tile([P, 2, PACK, N], F32, name="raw")
+            nc.sync.dma_start(raw[:], w2[2 * pair : 2 * pair + 2].rearrange("e (p j) n -> p e j n", j=PACK))
+            return raw
+
+        x_raw = {}
+        w1_raw = {}
+        w2_raw = {}
+        for u in range(2):
+            for c in range(T // CHUNK):
+                x_raw[u, c] = load_x(u, c)
+        gate_sb = keep.tile([P, SLOTS], F32, name="gate_sb")
+        for q in range(3):
+            w1_raw[2 * q] = load_w1(2 * q)
+            w1_raw[2 * q + 1] = load_w1(2 * q + 1)
+            w2_raw[q] = load_w2(q)
+            if q == 0:
+                nc.sync.dma_start(gate_sb[:], gate[0:P, :])
+
+        window = [keep.tile([P, T], F32, name=f"window{b}") for b in range(2)]
+        for b in range(2):
+            nc.gpsimd.memset(window[b][:], 0.0)
+
+        pairs = [keep.tile([P, T, 2], BF16, name=f"pairs{u}", align_bytes=64) for u in range(2)]
+        words = [pairs[u][:].rearrange("p t e -> p (t e)").bitcast(U32) for u in range(2)]
+        tokens = keep.tile([P, SLOTS, PACK], BF16, name="tokens", align_bytes=64)
+        token_words = tokens[:].rearrange("p s j -> p (s j)").bitcast(U32).rearrange("p (s u) -> p u s", u=2)
+        x_codes = keep.tile([P, SLOTS], U32, name="x_codes", align_bytes=64)
+        x_scales = keep.tile([P, SLOTS], U8, name="x_scales", align_bytes=64)
+
+        def cast_x(u, c, engine):
+            dst = pairs[u][:, c * CHUNK : (c + 1) * CHUNK, :]
+            src = x_raw[u, c][:].rearrange("p e t -> p t e")
+            copy(engine, dst, src)
+
+        def copy(engine, dst, src):
+            if engine == "v":
+                nc.vector.tensor_copy(dst, src)
+            else:
+                nc.scalar.copy(dst, src)
+
+        def gather(u, s0, s1):
+            nc.vector.tensor_copy(token_words[:, u, s0:s1], words[u].indirect(offsets[:, s0 // 16 : s1 // 16]))
+
+        def quantize(codes, scales, grouped):
+            nc.vector.quantize_mx(out=codes.bitcast(FP8X4), scales=scales, in_=grouped)
+
+        w1_codes = [keep.tile([P, 2 * H], U32, name=f"w1_codes{q}", align_bytes=64) for q in range(3)]
+        w1_scales = [keep.tile([P, 2 * H], U8, name=f"w1_scales{q}", align_bytes=64) for q in range(3)]
+        w2_codes = [keep.tile([P, 2 * N], U32, name=f"w2_codes{q}", align_bytes=64) for q in range(3)]
+        w2_scales = [keep.tile([P, 2 * N], U8, name=f"w2_scales{q}", align_bytes=64) for q in range(3)]
+
+        def group_w1(e, engine, dst):
+            copy(
+                engine,
+                dst.rearrange("p (t m j) -> p m j t", t=PACK, j=PACK),
+                w1_raw[e][:].rearrange("p j (m t) -> p m j t", t=PACK),
+            )
+
+        def prepare_w1(q, engines, joined):
+            grouped = work.tile([P, 2 * PACK * H], BF16, name="w1_grouped", align_bytes=64)
+            for half in range(2):
+                part = slice(half * PACK * H, (half + 1) * PACK * H)
+                group_w1(2 * q + half, engines[half], grouped[:, part])
+                if not joined:
+                    cols = slice(half * H, (half + 1) * H)
+                    quantize(w1_codes[q][:, cols], w1_scales[q][:, cols], grouped[:, part])
+            if joined:
+                quantize(w1_codes[q][:], w1_scales[q][:], grouped[:])
+
+        def prepare_w2(q, engine):
+            grouped = work.tile([P, PACK * 2 * N], BF16, name="w2_grouped", align_bytes=64)
+            copy(
+                engine,
+                grouped[:].rearrange("p (e c i j) -> p e c j i", e=2, i=4, j=PACK),
+                w2_raw[q][:].rearrange("p e j (c i) -> p e c j i", i=4),
+            )
+            quantize(w2_codes[q][:], w2_scales[q][:], grouped[:])
+
+        y = keep.tile([P, 2, SLOTS], F32, name="y")
+
+        def layer1(e, hidden):
+            q, place = e // 2, (e % 2) * C
+            for half in range(2):
+                cols = slice(e * C + half * HALF, e * C + (half + 1) * HALF)
+                acc = psum_h.tile([P, PACK, HALF], F32, name="acc_h")
+                for t in range(PACK):
+                    rows = slice((e % 2) * H + t * P, (e % 2) * H + (t + 1) * P)
+                    nc.tensor.matmul_mx(
+                        out=acc[:, t, :],
+                        lhsT=w1_codes[q][:, rows].bitcast(FP8X4),
+                        lhsT_scale=w1_scales[q][:, rows],
+                        rhs=x_codes[:, cols].bitcast(FP8X4),
+                        rhs_scale=x_scales[:, cols],
+                        start=True,
+                        stop=True,
+                    )
+                nc.scalar.activation(
+                    hidden[:, place + half * HALF : place + (half + 1) * HALF, :],
+                    acc[:].rearrange("p t n -> p n t"),
+                    SILU,
+                )
+
+        def layer2(e, h_codes, h_scales):
+            q, place = e // 2, (e % 2) * C
+            acc = psum_y.tile([P, 2, C], F32, name="acc_y")
+            for b in range(2):
+                rows = slice((e % 2) * N + b * P, (e % 2) * N + (b + 1) * P)
+                nc.tensor.matmul_mx(
+                    out=acc[:, b, :],
+                    lhsT=w2_codes[q][:, rows].bitcast(FP8X4),
+                    lhsT_scale=w2_scales[q][:, rows],
+                    rhs=h_codes[:, place : place + C].bitcast(FP8X4),
+                    rhs_scale=h_scales[:, place : place + C],
+                    start=True,
+                    stop=True,
+                )
+            nc.scalar.copy(y[:, :, e * C : (e + 1) * C], acc[:])
+
+        def pair(q, w1_engines, joined_w1, w2_engine, joined_h):
+            prepare_w1(q, w1_engines, joined_w1)
+            hidden = work.tile([P, 2 * C, PACK], BF16, name="hidden", align_bytes=64)
+            flat = hidden[:].rearrange("p s t -> p (s t)")
+            h_codes = work.tile([P, 2 * C], U32, name="h_codes", align_bytes=64)
+            h_scales = work.tile([P, 2 * C], U8, name="h_scales", align_bytes=64)
+            for half in range(2):
+                layer1(2 * q + half, hidden)
+                if not joined_h:
+                    cols = slice(half * C, (half + 1) * C)
+                    quantize(h_codes[:, cols], h_scales[:, cols], flat[:, half * PACK * C : (half + 1) * PACK * C])
+            if joined_h:
+                quantize(h_codes[:], h_scales[:], flat)
+            prepare_w2(q, w2_engine)
+            for half in range(2):
+                layer2(2 * q + half, h_codes, h_scales)
+
+        def scatter(b, g):
+            s0, s1 = PIECES[g]
+            nc.vector.tensor_tensor(
+                window[b][:].indirect(offsets[:, s0 // 16 : s1 // 16]), y[:, b, s0:s1], gate_sb[:, s0:s1], MULT
+            )
+
+        for u in range(2):
+            for c in range(3):
+                cast_x(u, c, "ssv"[c])
+            if u == 0:
+                gather(0, 0, SLOTS)
+        for s0, s1 in ((0, 512), (512, 1536)):
+            gather(1, s0, s1)
+            quantize(x_codes[:, s0:s1], x_scales[:, s0:s1], tokens[:, s0:s1, :].rearrange("p s j -> p (s j)"))
+        pair(0, "ss", False, "v", True)
+        pair(1, "ss", True, "s", True)
+        for b in range(2):
+            scatter(b, 0)
+        pair(2, "ss", True, "s", False)
+        for b in range(2):
+            scatter(b, 1)
+        for b in range(2):
+            scatter(b, 2)
+            nc.sync.dma_start(out[b * P : (b + 1) * P, :], window[b][:])

@@ -7,8 +7,8 @@ SLOTS = E * C
 P = 128
 PACK = 4
 GROUP = 512
-CHUNK = 1024
-PIECES = ((0, 512), (512, 1152), (1152, 1536))
+CHUNKS = ((0, 1024), (1024, 2048), (2048, 3072))
+
 HALF = 128
 
 FLOPS = 2 * SLOTS * H * (K + N)
@@ -27,7 +27,7 @@ def tile_routed_moe_kernel(tc, xT, w1, w2, gate, offs, out):
     nc = tc.nc
     with ExitStack() as ctx:
         keep = ctx.enter_context(tc.tile_pool(name="keep", bufs=1))
-        raws = ctx.enter_context(tc.tile_pool(name="raws", bufs=10))
+        raws = ctx.enter_context(tc.tile_pool(name="raws", bufs=5))
         work = ctx.enter_context(tc.tile_pool(name="work", bufs=2))
         psum_h = ctx.enter_context(tc.psum_pool(name="psum_h", bufs=4))
         psum_y = ctx.enter_context(tc.psum_pool(name="psum_y", bufs=2))
@@ -43,8 +43,9 @@ def tile_routed_moe_kernel(tc, xT, w1, w2, gate, offs, out):
         x_view = xT.rearrange("(p u e) n -> u p e n", u=2, e=2)
 
         def load_x(u, c):
-            raw = raws.tile([P, 2, CHUNK], F32, name="raw")
-            nc.sync.dma_start(raw[:], x_view[u, :, :, c * CHUNK : (c + 1) * CHUNK])
+            t0, t1 = CHUNKS[c]
+            raw = keep.tile([P, 2, t1 - t0], F32, name=f"x_raw{u}{c}")
+            nc.sync.dma_start(raw[:], x_view[u, :, :, t0:t1])
             return raw
 
         def load_w1(e):
@@ -61,15 +62,25 @@ def tile_routed_moe_kernel(tc, xT, w1, w2, gate, offs, out):
         w1_raw = {}
         w2_raw = {}
         for u in range(2):
-            for c in range(T // CHUNK):
+            for c in range(3):
                 x_raw[u, c] = load_x(u, c)
-        gate_sb = keep.tile([P, SLOTS], F32, name="gate_sb")
-        for q in range(3):
-            w1_raw[2 * q] = load_w1(2 * q)
-            w1_raw[2 * q + 1] = load_w1(2 * q + 1)
-            w2_raw[q] = load_w2(q)
-            if q == 0:
-                nc.sync.dma_start(gate_sb[:], gate[0:P, :])
+        gates = [keep.tile([P, GROUP], F32, name=f"gate{q}") for q in range(3)]
+
+        def load_gate(q):
+            nc.sync.dma_start(gates[q][:], gate[0:P, q * GROUP : (q + 1) * GROUP])
+
+        w1_raw[0] = load_w1(0)
+        w1_raw[1] = load_w1(1)
+        w2_raw[0] = load_w2(0)
+        w1_raw[2] = load_w1(2)
+        w2_raw[1] = load_w2(1)
+        w1_raw[3] = load_w1(3)
+        load_gate(0)
+        w1_raw[4] = load_w1(4)
+        load_gate(1)
+        w1_raw[5] = load_w1(5)
+        load_gate(2)
+        w2_raw[2] = load_w2(2)
 
         window = [keep.tile([P, T], F32, name=f"window{b}") for b in range(2)]
         for b in range(2):
@@ -83,9 +94,8 @@ def tile_routed_moe_kernel(tc, xT, w1, w2, gate, offs, out):
         x_scales = keep.tile([P, SLOTS], U8, name="x_scales", align_bytes=64)
 
         def cast_x(u, c, engine):
-            dst = pairs[u][:, c * CHUNK : (c + 1) * CHUNK, :]
-            src = x_raw[u, c][:].rearrange("p e t -> p t e")
-            copy(engine, dst, src)
+            t0, t1 = CHUNKS[c]
+            copy(engine, pairs[u][:, t0:t1, :], x_raw[u, c][:].rearrange("p e t -> p t e"))
 
         def copy(engine, dst, src):
             if engine == "v":
@@ -131,7 +141,7 @@ def tile_routed_moe_kernel(tc, xT, w1, w2, gate, offs, out):
             )
             quantize(w2_codes[q][:], w2_scales[q][:], grouped[:])
 
-        y = keep.tile([P, 2, SLOTS], F32, name="y")
+        y = [keep.tile([P, 2, GROUP], F32, name=f"y{q}") for q in range(3)]
 
         def layer1(e, hidden):
             q, place = e // 2, (e % 2) * C
@@ -169,7 +179,7 @@ def tile_routed_moe_kernel(tc, xT, w1, w2, gate, offs, out):
                     start=True,
                     stop=True,
                 )
-            nc.scalar.copy(y[:, :, e * C : (e + 1) * C], acc[:])
+            nc.scalar.copy(y[q][:, :, place : place + C], acc[:])
 
         def pair(q, w1_engines, joined_w1, w2_engine, joined_h):
             prepare_w1(q, w1_engines, joined_w1)
@@ -189,26 +199,25 @@ def tile_routed_moe_kernel(tc, xT, w1, w2, gate, offs, out):
                 layer2(2 * q + half, h_codes, h_scales)
 
         def scatter(b, g):
-            s0, s1 = PIECES[g]
+            s0, s1 = g * GROUP, (g + 1) * GROUP
             nc.vector.tensor_tensor(
-                window[b][:].indirect(offsets[:, s0 // 16 : s1 // 16]), y[:, b, s0:s1], gate_sb[:, s0:s1], MULT
+                window[b][:].indirect(offsets[:, s0 // 16 : s1 // 16]), y[g][:, b, :], gates[g][:], MULT
             )
 
         for u in range(2):
             for c in range(3):
                 cast_x(u, c, "ssv"[c])
-            if u == 0:
-                gather(0, 0, SLOTS)
+            gather(u, 0, SLOTS)
         for s0, s1 in ((0, 512), (512, 1536)):
-            gather(1, s0, s1)
             quantize(x_codes[:, s0:s1], x_scales[:, s0:s1], tokens[:, s0:s1, :].rearrange("p s j -> p (s j)"))
-        pair(0, "ss", False, "v", True)
-        pair(1, "ss", True, "s", True)
-        for b in range(2):
-            scatter(b, 0)
+        pair(0, "ss", False, "v", False)
+        pair(1, "sv", False, "v", False)
+        scatter(0, 0)
+        scatter(1, 0)
         pair(2, "ss", True, "s", False)
-        for b in range(2):
-            scatter(b, 1)
-        for b in range(2):
-            scatter(b, 2)
-            nc.sync.dma_start(out[b * P : (b + 1) * P, :], window[b][:])
+        scatter(0, 1)
+        scatter(1, 1)
+        scatter(0, 2)
+        nc.sync.dma_start(out[0:P, :], window[0][:])
+        scatter(1, 2)
+        nc.sync.dma_start(out[P : 2 * P, :], window[1][:])

@@ -7,7 +7,7 @@ SLOTS = E * C
 P = 128
 PACK = 4
 GROUP = 512
-CHUNKS = ((0, 1024), (1024, 2048), (2048, 3072))
+CHUNKS = ((0, 1024), (1024, 2048), (2048, 2560), (2560, 3072))
 
 HALF = 128
 
@@ -62,7 +62,7 @@ def tile_routed_moe_kernel(tc, xT, w1, w2, gate, offs, out):
         w1_raw = {}
         w2_raw = {}
         for u in range(2):
-            for c in range(3):
+            for c in range(4):
                 x_raw[u, c] = load_x(u, c)
         gates = [keep.tile([P, GROUP], F32, name=f"gate{q}") for q in range(3)]
 
@@ -72,15 +72,15 @@ def tile_routed_moe_kernel(tc, xT, w1, w2, gate, offs, out):
         w1_raw[0] = load_w1(0)
         w1_raw[1] = load_w1(1)
         w2_raw[0] = load_w2(0)
-        w1_raw[2] = load_w1(2)
         w2_raw[1] = load_w2(1)
+        w1_raw[2] = load_w1(2)
         w1_raw[3] = load_w1(3)
-        load_gate(0)
         w1_raw[4] = load_w1(4)
-        load_gate(1)
+        load_gate(0)
         w1_raw[5] = load_w1(5)
-        load_gate(2)
+        load_gate(1)
         w2_raw[2] = load_w2(2)
+        load_gate(2)
 
         window = [keep.tile([P, T], F32, name=f"window{b}") for b in range(2)]
         for b in range(2):
@@ -183,6 +183,7 @@ def tile_routed_moe_kernel(tc, xT, w1, w2, gate, offs, out):
 
         def pair(q, w1_engines, joined_w1, w2_engine, joined_h):
             prepare_w1(q, w1_engines, joined_w1)
+            prepare_w2(q, w2_engine)
             hidden = work.tile([P, 2 * C, PACK], BF16, name="hidden", align_bytes=64)
             flat = hidden[:].rearrange("p s t -> p (s t)")
             h_codes = work.tile([P, 2 * C], U32, name="h_codes", align_bytes=64)
@@ -194,7 +195,6 @@ def tile_routed_moe_kernel(tc, xT, w1, w2, gate, offs, out):
                     quantize(h_codes[:, cols], h_scales[:, cols], flat[:, half * PACK * C : (half + 1) * PACK * C])
             if joined_h:
                 quantize(h_codes[:], h_scales[:], flat)
-            prepare_w2(q, w2_engine)
             for half in range(2):
                 layer2(2 * q + half, h_codes, h_scales)
 
@@ -205,16 +205,16 @@ def tile_routed_moe_kernel(tc, xT, w1, w2, gate, offs, out):
             )
 
         for u in range(2):
-            for c in range(3):
-                cast_x(u, c, "ssv"[c])
+            for c in range(4):
+                cast_x(u, c, "ssvv"[c])
             gather(u, 0, SLOTS)
         for s0, s1 in ((0, 512), (512, 1536)):
             quantize(x_codes[:, s0:s1], x_scales[:, s0:s1], tokens[:, s0:s1, :].rearrange("p s j -> p (s j)"))
-        pair(0, "ss", False, "v", False)
-        pair(1, "sv", False, "v", False)
+        pair(0, "ss", False, "s", True)
+        pair(1, "sv", True, "v", True)
         scatter(0, 0)
         scatter(1, 0)
-        pair(2, "ss", True, "s", False)
+        pair(2, "ss", True, "s", True)
         scatter(0, 1)
         scatter(1, 1)
         scatter(0, 2)

from contextlib import ExitStack

import concourse.mybir as mybir

K, T, E, C, H, N = 512, 3072, 6, 256, 512, 256
SLOTS = E * C
P = 128
PACK = 4
GROUP = 512
CHUNKS = ((0, 1024), (1024, 2048), (2048, 2560), (2560, 3072))

HALF = 128

FLOPS = 2 * SLOTS * H * (K + N)

F32 = mybir.dt.float32
BF16 = mybir.dt.bfloat16
U32 = mybir.dt.uint32
U16 = mybir.dt.uint16
U8 = mybir.dt.uint8
FP8X4 = mybir.dt.float8_e4m3fn_x4
SILU = mybir.ActivationFunctionType.Silu
MULT = mybir.AluOpType.mult


def tile_routed_moe_kernel(tc, xT, w1, w2, gate, offs, out):
    nc = tc.nc
    with ExitStack() as ctx:
        keep = ctx.enter_context(tc.tile_pool(name="keep", bufs=1))
        raws = ctx.enter_context(tc.tile_pool(name="raws", bufs=5))
        work = ctx.enter_context(tc.tile_pool(name="work", bufs=2))
        psum_h = ctx.enter_context(tc.psum_pool(name="psum_h", bufs=4))
        psum_y = ctx.enter_context(tc.psum_pool(name="psum_y", bufs=2))

        offsets = keep.tile([P, SLOTS // 16], U16, name="offsets")
        nc.sync.dma_start(offsets[:], offs)

        warm_in = keep.tile([P, 8], F32, name="warm_in")
        warm_out = keep.tile([P, 8], F32, name="warm_out")
        nc.gpsimd.memset(warm_in[:], 0.0)
        nc.scalar.activation(warm_out[:], warm_in[:], SILU)

        x_view = xT.rearrange("(p u e) n -> u p e n", u=2, e=2)

        def load_x(u, c):
            t0, t1 = CHUNKS[c]
            raw = keep.tile([P, 2, t1 - t0], F32, name=f"x_raw{u}{c}")
            nc.sync.dma_start(raw[:], x_view[u, :, :, t0:t1])
            return raw

        def load_w1(e):
            raw = raws.tile([P, PACK, H], F32, name="raw")
            nc.sync.dma_start(raw[:], w1[e].rearrange("(p j) i -> p j i", j=PACK))
            return raw

        def load_w2(pair):
            raw = raws.tile([P, 2, PACK, N], F32, name="raw")
            nc.sync.dma_start(raw[:], w2[2 * pair : 2 * pair + 2].rearrange("e (p j) n -> p e j n", j=PACK))
            return raw

        x_raw = {}
        w1_raw = {}
        w2_raw = {}
        for u in range(2):
            for c in range(4):
                x_raw[u, c] = load_x(u, c)
        gates = [keep.tile([P, GROUP], F32, name=f"gate{q}") for q in range(3)]

        def load_gate(q):
            nc.sync.dma_start(gates[q][:], gate[0:P, q * GROUP : (q + 1) * GROUP])

        w1_raw[0] = load_w1(0)
        w1_raw[1] = load_w1(1)
        w2_raw[0] = load_w2(0)
        w2_raw[1] = load_w2(1)
        w1_raw[2] = load_w1(2)
        w1_raw[3] = load_w1(3)
        w1_raw[4] = load_w1(4)
        load_gate(0)
        w1_raw[5] = load_w1(5)
        load_gate(1)
        w2_raw[2] = load_w2(2)
        load_gate(2)

        window = [keep.tile([P, T], F32, name=f"window{b}") for b in range(2)]
        for b in range(2):
            nc.gpsimd.memset(window[b][:], 0.0)

        pairs = [keep.tile([P, T, 2], BF16, name=f"pairs{u}", align_bytes=64) for u in range(2)]
        words = [pairs[u][:].rearrange("p t e -> p (t e)").bitcast(U32) for u in range(2)]
        tokens = keep.tile([P, SLOTS, PACK], BF16, name="tokens", align_bytes=64)
        token_words = tokens[:].rearrange("p s j -> p (s j)").bitcast(U32).rearrange("p (s u) -> p u s", u=2)
        x_codes = keep.tile([P, SLOTS], U32, name="x_codes", align_bytes=64)
        x_scales = keep.tile([P, SLOTS], U8, name="x_scales", align_bytes=64)

        def cast_x(u, c, engine):
            t0, t1 = CHUNKS[c]
            copy(engine, pairs[u][:, t0:t1, :], x_raw[u, c][:].rearrange("p e t -> p t e"))

        def copy(engine, dst, src):
            if engine == "v":
                nc.vector.tensor_copy(dst, src)
            else:
                nc.scalar.copy(dst, src)

        def gather(u, s0, s1):
            nc.vector.tensor_copy(token_words[:, u, s0:s1], words[u].indirect(offsets[:, s0 // 16 : s1 // 16]))

        def quantize(codes, scales, grouped):
            nc.vector.quantize_mx(out=codes.bitcast(FP8X4), scales=scales, in_=grouped)

        w1_codes = [keep.tile([P, 2 * H], U32, name=f"w1_codes{q}", align_bytes=64) for q in range(3)]
        w1_scales = [keep.tile([P, 2 * H], U8, name=f"w1_scales{q}", align_bytes=64) for q in range(3)]
        w2_codes = [keep.tile([P, 2 * N], U32, name=f"w2_codes{q}", align_bytes=64) for q in range(3)]
        w2_scales = [keep.tile([P, 2 * N], U8, name=f"w2_scales{q}", align_bytes=64) for q in range(3)]

        def group_w1(e, engine, dst):
            copy(
                engine,
                dst.rearrange("p (t m j) -> p m j t", t=PACK, j=PACK),
                w1_raw[e][:].rearrange("p j (m t) -> p m j t", t=PACK),
            )

        def prepare_w1(q, engines, joined):
            grouped = work.tile([P, 2 * PACK * H], BF16, name="w1_grouped", align_bytes=64)
            for half in range(2):
                part = slice(half * PACK * H, (half + 1) * PACK * H)
                group_w1(2 * q + half, engines[half], grouped[:, part])
                if not joined:
                    cols = slice(half * H, (half + 1) * H)
                    quantize(w1_codes[q][:, cols], w1_scales[q][:, cols], grouped[:, part])
            if joined:
                quantize(w1_codes[q][:], w1_scales[q][:], grouped[:])

        def prepare_w2(q, engine):
            grouped = work.tile([P, PACK * 2 * N], BF16, name="w2_grouped", align_bytes=64)
            copy(
                engine,
                grouped[:].rearrange("p (e c i j) -> p e c j i", e=2, i=4, j=PACK),
                w2_raw[q][:].rearrange("p e j (c i) -> p e c j i", i=4),
            )
            quantize(w2_codes[q][:], w2_scales[q][:], grouped[:])

        y = [keep.tile([P, 2, GROUP], F32, name=f"y{q}") for q in range(3)]

        def layer1(e, hidden):
            q, place = e // 2, (e % 2) * C
            for half in range(2):
                cols = slice(e * C + half * HALF, e * C + (half + 1) * HALF)
                acc = psum_h.tile([P, PACK, HALF], F32, name="acc_h")
                for t in range(PACK):
                    rows = slice((e % 2) * H + t * P, (e % 2) * H + (t + 1) * P)
                    nc.tensor.matmul_mx(
                        out=acc[:, t, :],
                        lhsT=w1_codes[q][:, rows].bitcast(FP8X4),
                        lhsT_scale=w1_scales[q][:, rows],
                        rhs=x_codes[:, cols].bitcast(FP8X4),
                        rhs_scale=x_scales[:, cols],
                        start=True,
                        stop=True,
                    )
                nc.scalar.activation(
                    hidden[:, place + half * HALF : place + (half + 1) * HALF, :],
                    acc[:].rearrange("p t n -> p n t"),
                    SILU,
                )

        def layer2(e, h_codes, h_scales):
            q, place = e // 2, (e % 2) * C
            acc = psum_y.tile([P, 2, C], F32, name="acc_y")
            for b in range(2):
                rows = slice((e % 2) * N + b * P, (e % 2) * N + (b + 1) * P)
                nc.tensor.matmul_mx(
                    out=acc[:, b, :],
                    lhsT=w2_codes[q][:, rows].bitcast(FP8X4),
                    lhsT_scale=w2_scales[q][:, rows],
                    rhs=h_codes[:, place : place + C].bitcast(FP8X4),
                    rhs_scale=h_scales[:, place : place + C],
                    start=True,
                    stop=True,
                )
            nc.scalar.copy(y[q][:, :, place : place + C], acc[:])

        def pair(q, w1_engines, joined_w1, w2_engine, joined_h):
            prepare_w1(q, w1_engines, joined_w1)
            prepare_w2(q, w2_engine)
            hidden = work.tile([P, 2 * C, PACK], BF16, name="hidden", align_bytes=64)
            flat = hidden[:].rearrange("p s t -> p (s t)")
            h_codes = work.tile([P, 2 * C], U32, name="h_codes", align_bytes=64)
            h_scales = work.tile([P, 2 * C], U8, name="h_scales", align_bytes=64)
            for half in range(2):
                layer1(2 * q + half, hidden)
                if not joined_h:
                    cols = slice(half * C, (half + 1) * C)
                    quantize(h_codes[:, cols], h_scales[:, cols], flat[:, half * PACK * C : (half + 1) * PACK * C])
            if joined_h:
                quantize(h_codes[:], h_scales[:], flat)
            for half in range(2):
                layer2(2 * q + half, h_codes, h_scales)

        def scatter(b, g):
            s0, s1 = g * GROUP, (g + 1) * GROUP
            nc.vector.tensor_tensor(
                window[b][:].indirect(offsets[:, s0 // 16 : s1 // 16]), y[g][:, b, :], gates[g][:], MULT
            )

        for u in range(2):
            for c in range(4):
                cast_x(u, c, "ssvv"[c])
            gather(u, 0, SLOTS)
        for s0, s1 in ((0, 512), (512, 1536)):
            quantize(x_codes[:, s0:s1], x_scales[:, s0:s1], tokens[:, s0:s1, :].rearrange("p s j -> p (s j)"))
        pair(0, "ss", False, "s", True)
        pair(1, "sv", True, "v", True)
        scatter(0, 0)
        scatter(1, 0)
        pair(2, "ss", True, "s", True)
        scatter(0, 1)
        scatter(1, 1)
        scatter(0, 2)
        nc.sync.dma_start(out[0:P, :], window[0][:])
        scatter(1, 2)
        nc.sync.dma_start(out[P : 2 * P, :], window[1][:])
